import numpy as np
import ml_dtypes


def mxq(x, axis, fmt="e4m3"):
    dtype, down = {"e4m3": (ml_dtypes.float8_e4m3fn, 7), "e5m2": (ml_dtypes.float8_e5m2, 14)}[fmt]
    v = np.moveaxis(np.asarray(x, np.float32).astype(ml_dtypes.bfloat16).astype(np.float64), axis, -1)
    blocks = v.reshape(v.shape[:-1] + (-1, 32))
    amax = np.abs(blocks).max(-1, keepdims=True)
    byte = np.maximum(np.where(amax > 0, np.frexp(amax)[1] - 1 + 127, 0) - down, 1)
    scale = np.exp2(byte - 127.0)
    codes = (blocks / scale).astype(np.float32).astype(dtype).astype(np.float64)
    return np.moveaxis((codes * scale).reshape(v.shape), -1, axis)


WIDE = False


def mx_kscale(k):
    if not WIDE:
        return np.ones(k)
    levels = np.array([30, -30])
    if k % 512:
        return np.exp2(np.random.permutation(np.resize(levels, k // 32))).repeat(32)
    a = np.empty((k // 512, 16))
    for p in range(k // 512):
        a[p, :8] = np.random.permutation(np.resize(levels, 8))
        for g in range(8):
            far = levels[np.abs(levels - a[p, g]) >= 10]
            a[p, g + 8] = far[np.random.randint(len(far))]
    return np.exp2(a.ravel()).repeat(32)


def f64(x):
    return np.asarray(x).astype(np.float64)


def striped(idx):
    return np.tile(np.asarray(idx).reshape(-1, 16).T, (8, 1)).astype(np.uint16)


def unstriped(offs):
    return offs[:16].T.reshape(-1).astype(np.int64)


E2M1 = np.array([0.0, 0.5, 1.0, 1.5, 2.0, 3.0, 4.0, 6.0, -0.0, -0.5, -1.0, -1.5, -2.0, -3.0, -4.0, -6.0])


def pack_weight(w, fmt):
    k, n = w.shape
    w = f64(np.asarray(w, np.float32).astype(ml_dtypes.bfloat16)).reshape(k // 32, 32, n)
    amax = np.abs(w).max(1)
    if fmt in ("e4m3", "e5m2"):
        byte = np.frexp(amax)[1] - 1 + 127 - (7 if fmt == "e4m3" else 14)
    else:
        mant, ex = np.frexp(amax / 6.0)
        byte = np.where(mant > 0.5, ex, ex - 1) + 127
    byte = np.clip(np.where(amax > 0, byte, 1), 1, 254)
    scaled = (w * np.exp2(127.0 - byte)[:, None, :]).reshape(k, n).astype(np.float32)
    by_word = np.ascontiguousarray(scaled.reshape(k // 512, 128, 4, n).transpose(0, 1, 3, 2))
    if fmt in ("e4m3", "e5m2"):
        words = by_word.astype(ml_dtypes.float8_e4m3fn if fmt == "e4m3" else ml_dtypes.float8_e5m2).view(np.uint8)
    else:
        c = by_word.astype(ml_dtypes.float4_e2m1fn).view(np.uint8) & 0xF
        words = (c[..., 0::2] | (c[..., 1::2] << 4)).reshape(k // 512, 128, 2 * n)
    return np.ascontiguousarray(words), np.ascontiguousarray(byte.astype(np.uint8).reshape(k // 512, 16, n))


def unpack_weight(words, scales, fmt):
    g, _, n = scales.shape
    words = np.ascontiguousarray(words).reshape(g, 128, n, -1)
    if fmt in ("e4m3", "e5m2"):
        vals = words.view(ml_dtypes.float8_e4m3fn if fmt == "e4m3" else ml_dtypes.float8_e5m2).astype(np.float64)
    else:
        nib = np.empty((g, 128, n, 4), np.uint8)
        nib[..., 0::2] = words & 0xF
        nib[..., 1::2] = words >> 4
        vals = E2M1[nib]
    vals = vals * np.repeat(np.exp2(scales.astype(np.float64) - 127.0), 8, axis=1)[..., None]
    return vals.transpose(0, 1, 3, 2).reshape(g * 512, n)


def sigmoid(v):
    return 1.0 / (1.0 + np.exp(-v))


K, T, J, R, F, Z, C, O, N, L, E = 512, 1024, 256, 512, 512, 1024, 512, 128, 256, 512, 1024


def setup_inputs():
    n = np.random.standard_normal
    idx = np.random.permutation(T)[:J]
    idx2 = np.random.permutation(Z)[:J]
    idx3 = np.random.permutation(C)[:J]
    idx4 = np.random.permutation(C)[:O]
    idx5 = np.random.permutation(C)[:O]
    idx6 = np.random.permutation(J)[:O]
    idx7 = np.random.permutation(E)[:O]
    ff = mx_kscale(F)
    fk = mx_kscale(K)
    fr = mx_kscale(R)
    fl = mx_kscale(L)
    xop = pack_weight(n((F, Z)) / ff[:, None], "e2m1")
    wp = pack_weight(n((K, R)) * 1 / np.sqrt(K) / fk[:, None], "e2m1")
    w2p = pack_weight(n((F, R)) * 1 / np.sqrt(F) * ff[:, None], "e5m2")
    wbp = pack_weight(n((R, N)) * 1 / np.sqrt(R) / fr[:, None], "e5m2")
    sxp = pack_weight(n((L, O)) / fl[:, None], "e2m1")
    wsp = pack_weight(n((L, N)) * 1 / np.sqrt(L) * fl[:, None], "e5m2")
    return {
        "xo_words": xop[0],
        "xo_scales": xop[1],
        "cq": (np.random.randint(-7, 8, (K, T)).astype(np.float64)).astype(np.float32),
        "gs": (np.random.uniform(0.1, 0.4, (K, 1)) * fk[:, None]).astype(np.float32),
        "w_words": wp[0],
        "w_scales": wp[1],
        "w2_words": w2p[0],
        "w2_scales": w2p[1],
        "sa": (np.random.uniform(0.5, 1.6, (R, 1)) * fr[:, None]).astype(np.float32),
        "sb": (np.random.uniform(0.5, 1.6, (R, 1)) * fr[:, None]).astype(np.float32),
        "bg": (np.random.uniform(-2.0, 2.0, (R, 1))).astype(np.float32),
        "wb_words": wbp[0],
        "wb_scales": wbp[1],
        "sx_words": sxp[0],
        "sx_scales": sxp[1],
        "ws_words": wsp[0],
        "ws_scales": wsp[1],
        "offs": striped(idx),
        "offs2": striped(idx2),
        "offs3": striped(idx3),
        "offs4": striped(idx4),
        "offs5": striped(idx5),
        "offs6": striped(idx6),
        "offs7": striped(idx7),
    }


def reference(xo_words, xo_scales, cq, gs, w_words, w_scales, w2_words, w2_scales, sa, sb, bg, wb_words, wb_scales, sx_words, sx_scales, ws_words, ws_scales, offs, offs2, offs3, offs4, offs5, offs6, offs7):
    idx = unstriped(offs)
    idx2 = unstriped(offs2)
    idx3 = unstriped(offs3)
    idx4 = unstriped(offs4)
    idx5 = unstriped(offs5)
    idx6 = unstriped(offs6)
    idx7 = unstriped(offs7)
    xou = unpack_weight(xo_words, xo_scales, "e2m1")
    wu = unpack_weight(w_words, w_scales, "e2m1")
    w2u = unpack_weight(w2_words, w2_scales, "e5m2")
    wbu = unpack_weight(wb_words, wb_scales, "e5m2")
    sxu = unpack_weight(sx_words, sx_scales, "e2m1")
    wsu = unpack_weight(ws_words, ws_scales, "e5m2")
    x1 = f64(cq)[:, idx] * f64(gs)
    x1q = mxq(x1, 0, "e4m3")
    a = wu.T @ x1q
    xoidx2g = xou[:, idx2]
    b = w2u.T @ xoidx2g
    lb = b[:, 0:1]
    pw = np.zeros((R, C))
    pw[:, idx3] = a
    u1 = pw[:, idx4] * f64(sa) * sigmoid(pw[:, idx5] * lb + f64(bg))
    hid = np.maximum(u1, b[:, idx6] * f64(sb))
    hidq = mxq(hid, 0, "e4m3")
    p = wbu.T @ hidq + wsu.T @ sxu
    y = np.zeros((N, E))
    y[:, idx7] = p
    return y

@@ -1,0 +1,272 @@
+from contextlib import ExitStack
+
+import concourse.mybir as mybir
+
+K, T, J, R, F, Z, C, O, N, L, E = 512, 1024, 256, 512, 512, 1024, 512, 128, 256, 512, 1024
+FLOPS = 2 * (K * R * J + F * R * J + R * N * O + L * N * O)
+
+F32 = mybir.dt.float32
+BF16 = mybir.dt.bfloat16
+I32 = mybir.dt.int32
+U32 = mybir.dt.uint32
+U16 = mybir.dt.uint16
+U8 = mybir.dt.uint8
+E4M3 = mybir.dt.float8_e4m3fn_x4
+E5M2 = mybir.dt.float8_e5m2_x4
+E2M1 = mybir.dt.float4_e2m1fn_x4
+ACT = mybir.ActivationFunctionType
+ALU = mybir.AluOpType
+
+P = 128
+PACK = 4
+QUADS = 4
+QROWS = 4
+SCALAR_COLS = 4
+
+
+def tile_list_slopeboard_codednote_further_scattered_kernel(
+    tc, xo_words, xo_scales, cq, gs, w_words, w_scales, w2_words, w2_scales, sa, sb, bg,
+    wb_words, wb_scales, sx_words, sx_scales, ws_words, ws_scales,
+    offs, offs2, offs3, offs4, offs5, offs6, offs7, out,
+):
+    nc = tc.nc
+    with ExitStack() as ctx:
+        sb_pool = ctx.enter_context(tc.tile_pool(name="sbuf", bufs=1))
+        cq_pool = ctx.enter_context(tc.tile_pool(name="cq", bufs=1))
+        psum = ctx.enter_context(tc.psum_pool(name="psum", bufs=1))
+
+        def tile(name, shape, dtype):
+            return sb_pool.tile(shape, dtype, name=name, align_bytes=64)
+
+        def load_list(name, src):
+            lst = sb_pool.tile(list(src.shape), U16, name=name)
+            nc.sync.dma_start(lst[:], src)
+            return lst
+
+        def load_rows(name, src):
+            cols = tile(name, [P, PACK], F32)
+            nc.sync.dma_start(cols[:], src.rearrange("(p t) o -> p (t o)", t=PACK))
+            return cols
+
+        def load_words(name, src2d, dtype, width):
+            words = tile(name, [P, width], dtype)
+            nc.sync.dma_start(words[:].bitcast(I32), src2d.bitcast(I32))
+            return words
+
+        def staged_view(scales):
+            return scales[0].bitcast(I32).rearrange("(q r) w -> r q w", r=QROWS)
+
+        def load_cq(t):
+            rows = cq_pool.tile([P, T], F32, name=f"cq{t}", offset=4 * T * t)
+            nc.sync.dma_start(rows[:], cq.rearrange("(p t) c -> t p c", t=PACK)[t])
+            return rows
+
+        xo_plane = tile("xo_plane", [P, Z], U8)
+        nc.vector.memset(xo_plane[:].bitcast(I32), 0)
+        ww_plane = tile("ww_plane", [P, R], U8)
+        nc.vector.memset(ww_plane[:].bitcast(I32), 0)
+        late_plane = tile("late_plane", [P, 2 * N + O], U8)
+        nc.vector.memset(late_plane[:].bitcast(I32), 0)
+        board = [tile(f"board{t}", [P, C], F32) for t in range(PACK)]
+        for t in range(PACK):
+            nc.vector.memset(board[t][:], 0.0)
+        page = [tile(f"page{h}", [P, E], F32) for h in range(N // P)]
+        for h in range(N // P):
+            nc.vector.memset(page[h][:], 0.0)
+
+        xo_stage = tile("xo_stage", [QROWS, QUADS, Z // 4], I32)
+        nc.sync.dma_start(xo_stage[:], staged_view(xo_scales))
+        w2_stage = tile("w2_stage", [QROWS, QUADS, R // 4], I32)
+        nc.sync.dma_start(w2_stage[:], staged_view(w2_scales))
+        l2 = load_list("l2", offs2)
+        xo_raw = load_words("xo_raw", xo_words[0], U16, Z)
+        w2_raw = load_words("w2_raw", w2_words[0].rearrange("p n t -> p (n t)"), U32, R)
+        l1 = load_list("l1", offs)
+        cq_rows = [load_cq(0), load_cq(1)]
+        gs_cols = load_rows("gs_cols", gs)
+        w_stage = tile("w_stage", [QROWS, QUADS, R // 4], I32)
+        nc.sync.dma_start(w_stage[:], staged_view(w_scales))
+        w_raw = load_words("w_raw", w_words[0], U16, R)
+        cq_rows.append(load_cq(2))
+        cq_rows.append(load_cq(3))
+        l6 = load_list("l6", offs6)
+        sb_cols = load_rows("sb_cols", sb)
+        l3 = load_list("l3", offs3)
+        l5 = load_list("l5", offs5)
+        l4 = load_list("l4", offs4)
+        bg_cols = load_rows("bg_cols", bg)
+        sa_cols = load_rows("sa_cols", sa)
+        ws_sb = load_words("ws_sb", ws_words[0].rearrange("p n t -> p (n t)"), U32, N)
+        sx_sb = load_words("sx_sb", sx_words[0], U16, O)
+        wb_sb = load_words("wb_sb", wb_words[0].rearrange("p n t -> p (n t)"), U32, N)
+        l7 = load_list("l7", offs7)
+        for scales, col0, width in ((ws_scales, 0, N), (sx_scales, 2 * N, O), (wb_scales, N, N)):
+            for q in range(QUADS):
+                nc.sync.dma_start(
+                    late_plane[32 * q : 32 * q + QROWS, col0 : col0 + width].bitcast(I32),
+                    scales[0, QROWS * q : QROWS * (q + 1), :].bitcast(I32),
+                )
+
+        for q in range(QUADS):
+            nc.vector.tensor_copy(xo_plane[32 * q : 32 * q + QROWS, :].bitcast(I32), xo_stage[:, q, :])
+        for q in range(QUADS):
+            nc.vector.tensor_copy(ww_plane[32 * q : 32 * q + QROWS, :].bitcast(I32), w2_stage[:, q, :])
+        w2_dealt = tile("w2_dealt", [P, R], U32)
+        nc.scalar.copy(
+            w2_dealt[:].rearrange("p (t m) -> p m t", t=PACK), w2_raw[:].rearrange("p (m t) -> p m t", t=PACK)
+        )
+        xo_picked = tile("xo_picked", [P, J], U16)
+        nc.vector.tensor_copy(xo_picked[:], xo_raw[:].indirect(l2[:]))
+        xo_picked_sc = tile("xo_picked_sc", [P, J], U8)
+        nc.vector.tensor_copy(xo_picked_sc[:], xo_plane[:].indirect(l2[:]))
+        w2_dealt_sc = tile("w2_dealt_sc", [P, R], U8)
+        nc.vector.tensor_copy(
+            w2_dealt_sc[:].rearrange("p (t m) -> p t m", t=PACK), ww_plane[:].rearrange("p (m t) -> p t m", t=PACK)
+        )
+        for q in range(QUADS):
+            nc.vector.tensor_copy(ww_plane[32 * q : 32 * q + QROWS, :].bitcast(I32), w_stage[:, q, :])
+        w_dealt_sc = tile("w_dealt_sc", [P, R], U8)
+        nc.vector.tensor_copy(
+            w_dealt_sc[:].rearrange("p (t m) -> p t m", t=PACK), ww_plane[:].rearrange("p (m t) -> p t m", t=PACK)
+        )
+
+        x1_head = tile("x1_head", [P, PACK - 1, J], BF16)
+        x1_last = tile("x1_last", [P, J], BF16)
+
+        def pick_codes(t):
+            dst = x1_last[:] if t == PACK - 1 else x1_head[:, t, :]
+            nc.scalar.activation(out=dst, in_=cq_rows[t][:].indirect(l1[:]), func=ACT.Copy, scale=gs_cols[:, t : t + 1])
+
+        pick_codes(0)
+        w_dealt = tile("w_dealt", [P, R], U16)
+        nc.scalar.copy(
+            w_dealt[:].rearrange("p (t m) -> p m t", t=PACK), w_raw[:].rearrange("p (m t) -> p m t", t=PACK)
+        )
+        pick_codes(1)
+
+        b_banks = [psum.tile([P, 2, J], F32, name=f"b_bank{i}") for i in range(2)]
+        for t in range(PACK):
+            nc.tensor.matmul_mx(
+                out=b_banks[t // 2][:, t % 2, :],
+                lhsT=w2_dealt[:, t * P : (t + 1) * P].bitcast(E5M2),
+                lhsT_scale=w2_dealt_sc[:, t * P : (t + 1) * P],
+                rhs=xo_picked[:].bitcast(E2M1),
+                rhs_scale=xo_picked_sc[:],
+                start=True,
+                stop=True,
+            )
+        pick_codes(2)
+        x1_woven = cq_pool.tile([P, J, PACK], BF16, name="x1_woven", offset=4 * T * PACK, align_bytes=64)
+        nc.vector.tensor_copy(x1_woven[:, :, 0 : PACK - 1], x1_head[:].rearrange("p t j -> p j t"))
+        pick_codes(3)
+        x1_codes = tile("x1_codes", [P, J], U32)
+        x1_scales = tile("x1_scales", [P, J], U8)
+        halves = [slice(0, J // 2), slice(J // 2, J)]
+        for cols in halves:
+            nc.vector.tensor_copy(x1_woven[:, cols, PACK - 1], x1_last[:, cols])
+        for cols in halves:
+            nc.vector.quantize_mx(
+                out=x1_codes[:, cols].bitcast(E4M3),
+                scales=x1_scales[:, cols],
+                in_=x1_woven[:, cols, :].rearrange("p j t -> p (j t)"),
+            )
+
+        b_offsets = [4 * T * PACK, 4 * T * PACK + 4 * J, 4 * T * (PACK - 1), 4 * T * (PACK - 1) + 4 * J]
+        b_rows = [cq_pool.tile([P, J], F32, name=f"b_rows{t}", offset=b_offsets[t]) for t in range(PACK)]
+        for t in (0, 1):
+            nc.vector.tensor_copy(b_rows[t][:], b_banks[0][:, t, :])
+        for t in (2, 3):
+            nc.scalar.copy(b_rows[t][:], b_banks[1][:, t - 2, :])
+
+        b_picked = tile("b_picked", [P, PACK, O], F32)
+        for t in (2, 3, 0, 1):
+            nc.scalar.activation(
+                out=b_picked[:, t, :], in_=b_rows[t][:].indirect(l6[:]), func=ACT.Copy, scale=sb_cols[:, t : t + 1]
+            )
+
+        a_banks = [psum.tile([P, J], F32, name=f"a_bank{t}", tag=f"bank{t}") for t in range(PACK)]
+        for t in range(PACK):
+            nc.tensor.matmul_mx(
+                out=a_banks[t][:],
+                lhsT=w_dealt[:, t * P : (t + 1) * P].bitcast(E2M1),
+                lhsT_scale=w_dealt_sc[:, t * P : (t + 1) * P],
+                rhs=x1_codes[:].bitcast(E4M3),
+                rhs_scale=x1_scales[:],
+                start=True,
+                stop=True,
+            )
+        a_rows = [tile(f"a_rows{t}", [P, J], F32) for t in range(PACK)]
+        nc.vector.tensor_copy(a_rows[0][:], a_banks[0][:])
+        for t in range(1, PACK):
+            nc.scalar.copy(a_rows[t][:], a_banks[t][:])
+
+        p_banks = [psum.tile([P, O], F32, name=f"p_bank{h}", tag=f"bank{h}") for h in range(N // P)]
+        for h in range(N // P):
+            nc.tensor.matmul_mx(
+                out=p_banks[h][:],
+                lhsT=ws_sb[:, h * P : (h + 1) * P].bitcast(E5M2),
+                lhsT_scale=late_plane[:, h * P : (h + 1) * P],
+                rhs=sx_sb[:].bitcast(E2M1),
+                rhs_scale=late_plane[:, 2 * N : 2 * N + O],
+                start=True,
+                stop=False,
+            )
+
+        split = 16 * SCALAR_COLS
+        nc.vector.tensor_copy(board[0][:].indirect(l3[:]), a_rows[0][:])
+        nc.scalar.activation(out=board[1][:].indirect(l3[:]), in_=a_rows[1][:], func=ACT.Copy)
+        nc.vector.tensor_copy(board[2][:].indirect(l3[:]), a_rows[2][:])
+        nc.scalar.activation(out=board[3][:].indirect(l3[:, 0:SCALAR_COLS]), in_=a_rows[3][:, 0:split], func=ACT.Copy)
+        nc.vector.tensor_copy(board[3][:].indirect(l3[:, SCALAR_COLS : J // 16]), a_rows[3][:, split:J])
+
+        gate = tile("gate", [P, PACK, O], F32)
+        scaled = tile("scaled", [P, PACK, O], F32)
+        for t in range(PACK):
+            nc.scalar.activation(
+                out=gate[:, t, :], in_=board[t][:].indirect(l5[:]), func=ACT.Sigmoid,
+                bias=bg_cols[:, t : t + 1], scale=b_rows[t][:, 0:1],
+            )
+            nc.scalar.activation(
+                out=scaled[:, t, :], in_=board[t][:].indirect(l4[:]), func=ACT.Copy, scale=sa_cols[:, t : t + 1]
+            )
+
+        u1 = tile("u1", [P, PACK, O], F32)
+        hid = tile("hid", [P, O, PACK], BF16)
+
+        def gated(ts):
+            nc.vector.tensor_tensor(u1[:, ts, :], scaled[:, ts, :], gate[:, ts, :], ALU.mult)
+
+        def larger(ts):
+            nc.vector.tensor_tensor(
+                hid[:, :, ts], u1[:, ts, :].rearrange("p t o -> p o t"),
+                b_picked[:, ts, :].rearrange("p t o -> p o t"), ALU.max,
+            )
+
+        gated(slice(0, 2))
+        gated(slice(2, 3))
+        larger(slice(0, 2))
+        gated(slice(3, 4))
+        larger(slice(2, 4))
+        hid_codes = tile("hid_codes", [P, O], U32)
+        hid_scales = tile("hid_scales", [P, O], U8)
+        nc.vector.quantize_mx(
+            out=hid_codes[:].bitcast(E4M3), scales=hid_scales[:], in_=hid[:].rearrange("p o t -> p (o t)")
+        )
+        for h in range(N // P):
+            nc.tensor.matmul_mx(
+                out=p_banks[h][:],
+                lhsT=wb_sb[:, h * P : (h + 1) * P].bitcast(E5M2),
+                lhsT_scale=late_plane[:, N + h * P : N + (h + 1) * P],
+                rhs=hid_codes[:].bitcast(E4M3),
+                rhs_scale=hid_scales[:],
+                start=False,
+                stop=True,
+            )
+
+        p_rows = [tile(f"p_rows{h}", [P, O], F32) for h in range(N // P)]
+        nc.vector.tensor_copy(p_rows[0][:], p_banks[0][:])
+        nc.scalar.copy(p_rows[1][:], p_banks[1][:])
+        nc.vector.tensor_copy(page[0][:].indirect(l7[:]), p_rows[0][:])
+        nc.scalar.activation(out=page[1][:].indirect(l7[:]), in_=p_rows[1][:], func=ACT.Copy)
+        nc.sync.dma_start(out[0:P, :], page[0][:])
+        nc.scalar.dma_start(out[P:N, :], page[1][:])

@@ -61,6 +61,10 @@ def tile_list_slopeboard_codednote_further_scattered_kernel(
             nc.sync.dma_start(rows[:], cq.rearrange("(p t) c -> t p c", t=PACK)[t])
             return rows
 
+        warm_in = tile("warm_in", [P, 1], F32)
+        nc.vector.memset(warm_in[:], 0.0)
+        warm_out = tile("warm_out", [P, 1], F32)
+        nc.scalar.activation(out=warm_out[:], in_=warm_in[:], func=ACT.Sigmoid)
         xo_plane = tile("xo_plane", [P, Z], U8)
         nc.vector.memset(xo_plane[:].bitcast(I32), 0)
         ww_plane = tile("ww_plane", [P, R], U8)

from contextlib import ExitStack

import concourse.mybir as mybir

K, T, J, R, F, Z, C, O, N, L, E = 512, 1024, 256, 512, 512, 1024, 512, 128, 256, 512, 1024
FLOPS = 2 * (K * R * J + F * R * J + R * N * O + L * N * O)

F32 = mybir.dt.float32
BF16 = mybir.dt.bfloat16
I32 = mybir.dt.int32
U32 = mybir.dt.uint32
U16 = mybir.dt.uint16
U8 = mybir.dt.uint8
E4M3 = mybir.dt.float8_e4m3fn_x4
E5M2 = mybir.dt.float8_e5m2_x4
E2M1 = mybir.dt.float4_e2m1fn_x4
ACT = mybir.ActivationFunctionType
ALU = mybir.AluOpType

P = 128
PACK = 4
QUADS = 4
QROWS = 4
SCALAR_COLS = 4


def tile_list_slopeboard_codednote_further_scattered_kernel(
    tc, xo_words, xo_scales, cq, gs, w_words, w_scales, w2_words, w2_scales, sa, sb, bg,
    wb_words, wb_scales, sx_words, sx_scales, ws_words, ws_scales,
    offs, offs2, offs3, offs4, offs5, offs6, offs7, out,
):
    nc = tc.nc
    with ExitStack() as ctx:
        sb_pool = ctx.enter_context(tc.tile_pool(name="sbuf", bufs=1))
        cq_pool = ctx.enter_context(tc.tile_pool(name="cq", bufs=1))
        psum = ctx.enter_context(tc.psum_pool(name="psum", bufs=1))

        def tile(name, shape, dtype):
            return sb_pool.tile(shape, dtype, name=name, align_bytes=64)

        def load_list(name, src):
            lst = sb_pool.tile(list(src.shape), U16, name=name)
            nc.sync.dma_start(lst[:], src)
            return lst

        def load_rows(name, src):
            cols = tile(name, [P, PACK], F32)
            nc.sync.dma_start(cols[:], src.rearrange("(p t) o -> p (t o)", t=PACK))
            return cols

        def load_words(name, src2d, dtype, width):
            words = tile(name, [P, width], dtype)
            nc.sync.dma_start(words[:].bitcast(I32), src2d.bitcast(I32))
            return words

        def staged_view(scales):
            return scales[0].bitcast(I32).rearrange("(q r) w -> r q w", r=QROWS)

        def load_cq(t):
            rows = cq_pool.tile([P, T], F32, name=f"cq{t}", offset=4 * T * t)
            nc.sync.dma_start(rows[:], cq.rearrange("(p t) c -> t p c", t=PACK)[t])
            return rows

        warm_in = tile("warm_in", [P, 1], F32)
        nc.vector.memset(warm_in[:], 0.0)
        warm_out = tile("warm_out", [P, 1], F32)
        nc.scalar.activation(out=warm_out[:], in_=warm_in[:], func=ACT.Sigmoid)
        xo_plane = tile("xo_plane", [P, Z], U8)
        nc.vector.memset(xo_plane[:].bitcast(I32), 0)
        ww_plane = tile("ww_plane", [P, R], U8)
        nc.vector.memset(ww_plane[:].bitcast(I32), 0)
        late_plane = tile("late_plane", [P, 2 * N + O], U8)
        nc.vector.memset(late_plane[:].bitcast(I32), 0)
        board = [tile(f"board{t}", [P, C], F32) for t in range(PACK)]
        for t in range(PACK):
            nc.vector.memset(board[t][:], 0.0)
        page = [tile(f"page{h}", [P, E], F32) for h in range(N // P)]
        for h in range(N // P):
            nc.vector.memset(page[h][:], 0.0)

        xo_stage = tile("xo_stage", [QROWS, QUADS, Z // 4], I32)
        nc.sync.dma_start(xo_stage[:], staged_view(xo_scales))
        w2_stage = tile("w2_stage", [QROWS, QUADS, R // 4], I32)
        nc.sync.dma_start(w2_stage[:], staged_view(w2_scales))
        l2 = load_list("l2", offs2)
        xo_raw = load_words("xo_raw", xo_words[0], U16, Z)
        w2_raw = load_words("w2_raw", w2_words[0].rearrange("p n t -> p (n t)"), U32, R)
        l1 = load_list("l1", offs)
        cq_rows = [load_cq(0), load_cq(1)]
        gs_cols = load_rows("gs_cols", gs)
        w_stage = tile("w_stage", [QROWS, QUADS, R // 4], I32)
        nc.sync.dma_start(w_stage[:], staged_view(w_scales))
        w_raw = load_words("w_raw", w_words[0], U16, R)
        cq_rows.append(load_cq(2))
        cq_rows.append(load_cq(3))
        l6 = load_list("l6", offs6)
        sb_cols = load_rows("sb_cols", sb)
        l3 = load_list("l3", offs3)
        l5 = load_list("l5", offs5)
        l4 = load_list("l4", offs4)
        bg_cols = load_rows("bg_cols", bg)
        sa_cols = load_rows("sa_cols", sa)
        ws_sb = load_words("ws_sb", ws_words[0].rearrange("p n t -> p (n t)"), U32, N)
        sx_sb = load_words("sx_sb", sx_words[0], U16, O)
        wb_sb = load_words("wb_sb", wb_words[0].rearrange("p n t -> p (n t)"), U32, N)
        l7 = load_list("l7", offs7)
        for scales, col0, width in ((ws_scales, 0, N), (sx_scales, 2 * N, O), (wb_scales, N, N)):
            for q in range(QUADS):
                nc.sync.dma_start(
                    late_plane[32 * q : 32 * q + QROWS, col0 : col0 + width].bitcast(I32),
                    scales[0, QROWS * q : QROWS * (q + 1), :].bitcast(I32),
                )

        for q in range(QUADS):
            nc.vector.tensor_copy(xo_plane[32 * q : 32 * q + QROWS, :].bitcast(I32), xo_stage[:, q, :])
        for q in range(QUADS):
            nc.vector.tensor_copy(ww_plane[32 * q : 32 * q + QROWS, :].bitcast(I32), w2_stage[:, q, :])
        w2_dealt = tile("w2_dealt", [P, R], U32)
        nc.scalar.copy(
            w2_dealt[:].rearrange("p (t m) -> p m t", t=PACK), w2_raw[:].rearrange("p (m t) -> p m t", t=PACK)
        )
        xo_picked = tile("xo_picked", [P, J], U16)
        nc.vector.tensor_copy(xo_picked[:], xo_raw[:].indirect(l2[:]))
        xo_picked_sc = tile("xo_picked_sc", [P, J], U8)
        nc.vector.tensor_copy(xo_picked_sc[:], xo_plane[:].indirect(l2[:]))
        w2_dealt_sc = tile("w2_dealt_sc", [P, R], U8)
        nc.vector.tensor_copy(
            w2_dealt_sc[:].rearrange("p (t m) -> p t m", t=PACK), ww_plane[:].rearrange("p (m t) -> p t m", t=PACK)
        )
        for q in range(QUADS):
            nc.vector.tensor_copy(ww_plane[32 * q : 32 * q + QROWS, :].bitcast(I32), w_stage[:, q, :])
        w_dealt_sc = tile("w_dealt_sc", [P, R], U8)
        nc.vector.tensor_copy(
            w_dealt_sc[:].rearrange("p (t m) -> p t m", t=PACK), ww_plane[:].rearrange("p (m t) -> p t m", t=PACK)
        )

        x1_head = tile("x1_head", [P, PACK - 1, J], BF16)
        x1_last = tile("x1_last", [P, J], BF16)

        def pick_codes(t):
            dst = x1_last[:] if t == PACK - 1 else x1_head[:, t, :]
            nc.scalar.activation(out=dst, in_=cq_rows[t][:].indirect(l1[:]), func=ACT.Copy, scale=gs_cols[:, t : t + 1])

        pick_codes(0)
        w_dealt = tile("w_dealt", [P, R], U16)
        nc.scalar.copy(
            w_dealt[:].rearrange("p (t m) -> p m t", t=PACK), w_raw[:].rearrange("p (m t) -> p m t", t=PACK)
        )
        pick_codes(1)

        b_banks = [psum.tile([P, 2, J], F32, name=f"b_bank{i}") for i in range(2)]
        for t in range(PACK):
            nc.tensor.matmul_mx(
                out=b_banks[t // 2][:, t % 2, :],
                lhsT=w2_dealt[:, t * P : (t + 1) * P].bitcast(E5M2),
                lhsT_scale=w2_dealt_sc[:, t * P : (t + 1) * P],
                rhs=xo_picked[:].bitcast(E2M1),
                rhs_scale=xo_picked_sc[:],
                start=True,
                stop=True,
            )
        pick_codes(2)
        x1_woven = cq_pool.tile([P, J, PACK], BF16, name="x1_woven", offset=4 * T * PACK, align_bytes=64)
        nc.vector.tensor_copy(x1_woven[:, :, 0 : PACK - 1], x1_head[:].rearrange("p t j -> p j t"))
        pick_codes(3)
        x1_codes = tile("x1_codes", [P, J], U32)
        x1_scales = tile("x1_scales", [P, J], U8)
        halves = [slice(0, J // 2), slice(J // 2, J)]
        for cols in halves:
            nc.vector.tensor_copy(x1_woven[:, cols, PACK - 1], x1_last[:, cols])
        for cols in halves:
            nc.vector.quantize_mx(
                out=x1_codes[:, cols].bitcast(E4M3),
                scales=x1_scales[:, cols],
                in_=x1_woven[:, cols, :].rearrange("p j t -> p (j t)"),
            )

        b_offsets = [4 * T * PACK, 4 * T * PACK + 4 * J, 4 * T * (PACK - 1), 4 * T * (PACK - 1) + 4 * J]
        b_rows = [cq_pool.tile([P, J], F32, name=f"b_rows{t}", offset=b_offsets[t]) for t in range(PACK)]
        for t in (0, 1):
            nc.vector.tensor_copy(b_rows[t][:], b_banks[0][:, t, :])
        for t in (2, 3):
            nc.scalar.copy(b_rows[t][:], b_banks[1][:, t - 2, :])

        b_picked = tile("b_picked", [P, PACK, O], F32)
        for t in (2, 3, 0, 1):
            nc.scalar.activation(
                out=b_picked[:, t, :], in_=b_rows[t][:].indirect(l6[:]), func=ACT.Copy, scale=sb_cols[:, t : t + 1]
            )

        a_banks = [psum.tile([P, J], F32, name=f"a_bank{t}", tag=f"bank{t}") for t in range(PACK)]
        for t in range(PACK):
            nc.tensor.matmul_mx(
                out=a_banks[t][:],
                lhsT=w_dealt[:, t * P : (t + 1) * P].bitcast(E2M1),
                lhsT_scale=w_dealt_sc[:, t * P : (t + 1) * P],
                rhs=x1_codes[:].bitcast(E4M3),
                rhs_scale=x1_scales[:],
                start=True,
                stop=True,
            )
        a_rows = [tile(f"a_rows{t}", [P, J], F32) for t in range(PACK)]
        nc.vector.tensor_copy(a_rows[0][:], a_banks[0][:])
        for t in range(1, PACK):
            nc.scalar.copy(a_rows[t][:], a_banks[t][:])

        p_banks = [psum.tile([P, O], F32, name=f"p_bank{h}", tag=f"bank{h}") for h in range(N // P)]
        for h in range(N // P):
            nc.tensor.matmul_mx(
                out=p_banks[h][:],
                lhsT=ws_sb[:, h * P : (h + 1) * P].bitcast(E5M2),
                lhsT_scale=late_plane[:, h * P : (h + 1) * P],
                rhs=sx_sb[:].bitcast(E2M1),
                rhs_scale=late_plane[:, 2 * N : 2 * N + O],
                start=True,
                stop=False,
            )

        split = 16 * SCALAR_COLS
        nc.vector.tensor_copy(board[0][:].indirect(l3[:]), a_rows[0][:])
        nc.scalar.activation(out=board[1][:].indirect(l3[:]), in_=a_rows[1][:], func=ACT.Copy)
        nc.vector.tensor_copy(board[2][:].indirect(l3[:]), a_rows[2][:])
        nc.scalar.activation(out=board[3][:].indirect(l3[:, 0:SCALAR_COLS]), in_=a_rows[3][:, 0:split], func=ACT.Copy)
        nc.vector.tensor_copy(board[3][:].indirect(l3[:, SCALAR_COLS : J // 16]), a_rows[3][:, split:J])

        gate = tile("gate", [P, PACK, O], F32)
        scaled = tile("scaled", [P, PACK, O], F32)
        for t in range(PACK):
            nc.scalar.activation(
                out=gate[:, t, :], in_=board[t][:].indirect(l5[:]), func=ACT.Sigmoid,
                bias=bg_cols[:, t : t + 1], scale=b_rows[t][:, 0:1],
            )
            nc.scalar.activation(
                out=scaled[:, t, :], in_=board[t][:].indirect(l4[:]), func=ACT.Copy, scale=sa_cols[:, t : t + 1]
            )

        u1 = tile("u1", [P, PACK, O], F32)
        hid = tile("hid", [P, O, PACK], BF16)

        def gated(ts):
            nc.vector.tensor_tensor(u1[:, ts, :], scaled[:, ts, :], gate[:, ts, :], ALU.mult)

        def larger(ts):
            nc.vector.tensor_tensor(
                hid[:, :, ts], u1[:, ts, :].rearrange("p t o -> p o t"),
                b_picked[:, ts, :].rearrange("p t o -> p o t"), ALU.max,
            )

        gated(slice(0, 2))
        gated(slice(2, 3))
        larger(slice(0, 2))
        gated(slice(3, 4))
        larger(slice(2, 4))
        hid_codes = tile("hid_codes", [P, O], U32)
        hid_scales = tile("hid_scales", [P, O], U8)
        nc.vector.quantize_mx(
            out=hid_codes[:].bitcast(E4M3), scales=hid_scales[:], in_=hid[:].rearrange("p o t -> p (o t)")
        )
        for h in range(N // P):
            nc.tensor.matmul_mx(
                out=p_banks[h][:],
                lhsT=wb_sb[:, h * P : (h + 1) * P].bitcast(E5M2),
                lhsT_scale=late_plane[:, N + h * P : N + (h + 1) * P],
                rhs=hid_codes[:].bitcast(E4M3),
                rhs_scale=hid_scales[:],
                start=False,
                stop=True,
            )

        p_rows = [tile(f"p_rows{h}", [P, O], F32) for h in range(N // P)]
        nc.vector.tensor_copy(p_rows[0][:], p_banks[0][:])
        nc.scalar.copy(p_rows[1][:], p_banks[1][:])
        nc.vector.tensor_copy(page[0][:].indirect(l7[:]), p_rows[0][:])
        nc.scalar.activation(out=page[1][:].indirect(l7[:]), in_=p_rows[1][:], func=ACT.Copy)
        nc.sync.dma_start(out[0:P, :], page[0][:])
        nc.scalar.dma_start(out[P:N, :], page[1][:])
